import numpy as np
import ml_dtypes


def mxq(x, axis, fmt="e4m3"):
    dtype, down = {"e4m3": (ml_dtypes.float8_e4m3fn, 7), "e5m2": (ml_dtypes.float8_e5m2, 14)}[fmt]
    v = np.moveaxis(np.asarray(x, np.float32).astype(ml_dtypes.bfloat16).astype(np.float64), axis, -1)
    blocks = v.reshape(v.shape[:-1] + (-1, 32))
    amax = np.abs(blocks).max(-1, keepdims=True)
    byte = np.maximum(np.where(amax > 0, np.frexp(amax)[1] - 1 + 127, 0) - down, 1)
    scale = np.exp2(byte - 127.0)
    codes = (blocks / scale).astype(np.float32).astype(dtype).astype(np.float64)
    return np.moveaxis((codes * scale).reshape(v.shape), -1, axis)


WIDE = False


def mx_kscale(k):
    if not WIDE:
        return np.ones(k)
    levels = np.array([30, -30])
    if k % 512:
        return np.exp2(np.random.permutation(np.resize(levels, k // 32))).repeat(32)
    a = np.empty((k // 512, 16))
    for p in range(k // 512):
        a[p, :8] = np.random.permutation(np.resize(levels, 8))
        for g in range(8):
            far = levels[np.abs(levels - a[p, g]) >= 10]
            a[p, g + 8] = far[np.random.randint(len(far))]
    return np.exp2(a.ravel()).repeat(32)


def f64(x):
    return np.asarray(x).astype(np.float64)


def striped(idx):
    return np.tile(np.asarray(idx).reshape(-1, 16).T, (8, 1)).astype(np.uint16)


def unstriped(offs):
    return offs[:16].T.reshape(-1).astype(np.int64)


E2M1 = np.array([0.0, 0.5, 1.0, 1.5, 2.0, 3.0, 4.0, 6.0, -0.0, -0.5, -1.0, -1.5, -2.0, -3.0, -4.0, -6.0])


def pack_weight(w, fmt):
    k, n = w.shape
    w = f64(np.asarray(w, np.float32).astype(ml_dtypes.bfloat16)).reshape(k // 32, 32, n)
    amax = np.abs(w).max(1)
    if fmt in ("e4m3", "e5m2"):
        byte = np.frexp(amax)[1] - 1 + 127 - (7 if fmt == "e4m3" else 14)
    else:
        mant, ex = np.frexp(amax / 6.0)
        byte = np.where(mant > 0.5, ex, ex - 1) + 127
    byte = np.clip(np.where(amax > 0, byte, 1), 1, 254)
    scaled = (w * np.exp2(127.0 - byte)[:, None, :]).reshape(k, n).astype(np.float32)
    by_word = np.ascontiguousarray(scaled.reshape(k // 512, 128, 4, n).transpose(0, 1, 3, 2))
    if fmt in ("e4m3", "e5m2"):
        words = by_word.astype(ml_dtypes.float8_e4m3fn if fmt == "e4m3" else ml_dtypes.float8_e5m2).view(np.uint8)
    else:
        c = by_word.astype(ml_dtypes.float4_e2m1fn).view(np.uint8) & 0xF
        words = (c[..., 0::2] | (c[..., 1::2] << 4)).reshape(k // 512, 128, 2 * n)
    return np.ascontiguousarray(words), np.ascontiguousarray(byte.astype(np.uint8).reshape(k // 512, 16, n))


def unpack_weight(words, scales, fmt):
    g, _, n = scales.shape
    words = np.ascontiguousarray(words).reshape(g, 128, n, -1)
    if fmt in ("e4m3", "e5m2"):
        vals = words.view(ml_dtypes.float8_e4m3fn if fmt == "e4m3" else ml_dtypes.float8_e5m2).astype(np.float64)
    else:
        nib = np.empty((g, 128, n, 4), np.uint8)
        nib[..., 0::2] = words & 0xF
        nib[..., 1::2] = words >> 4
        vals = E2M1[nib]
    vals = vals * np.repeat(np.exp2(scales.astype(np.float64) - 127.0), 8, axis=1)[..., None]
    return vals.transpose(0, 1, 3, 2).reshape(g * 512, n)


def bf(x):
    return np.asarray(x, np.float32).astype(ml_dtypes.bfloat16)


def planes(Y):
    r, m = Y.shape
    b = f64(bf(Y)).reshape(r // 32, 32, m)
    amax = np.abs(b).max(1)
    byte = np.clip(np.where(amax > 0, np.frexp(amax)[1] - 1 + 127 - 7, 1), 1, 254)
    codes = (b * np.exp2(127.0 - byte)[:, None, :]).reshape(r, m).astype(np.float32).astype(ml_dtypes.float8_e4m3fn).view(np.uint8)
    words = codes.reshape(r // 512, 128, 4, m).transpose(0, 1, 3, 2)
    return np.ascontiguousarray(words), np.ascontiguousarray(byte.astype(np.uint8).reshape(r // 512, 16, m))


K, T, J, R, O, N, Z = 512, 512, 256, 512, 128, 512, 512


def setup_inputs():
    n = np.random.standard_normal
    idx = np.random.permutation(T)[:J]
    idx2 = np.random.permutation(J)[:O]
    idx3 = np.random.permutation(J)[:O]
    idx4 = np.random.permutation(Z)[:O]
    fk = mx_kscale(K)
    fr = mx_kscale(R)
    wp = pack_weight(n((K, R)) * 1 / np.sqrt(K) * fk[:, None] * fr, "e5m2")
    wbp = pack_weight(n((R, N)) * 1 / np.sqrt(R) / fr[:, None], "e2m1")
    return {
        "xf": (n((K, T))).astype(np.float32),
        "ow": (n((K, J)) * 0.7).astype(np.float32),
        "fk": (np.random.uniform(0.5, 2.0, (K, 1)) / fk[:, None]).astype(np.float32),
        "w_words": wp[0],
        "w_scales": wp[1],
        "wb_words": wbp[0],
        "wb_scales": wbp[1],
        "tz": (n((N, Z))).astype(np.float32),
        "offs": striped(idx),
        "offs2": striped(idx2),
        "offs3": striped(idx3),
        "offs4": striped(idx4),
    }


def reference(xf, ow, fk, w_words, w_scales, wb_words, wb_scales, tz, offs, offs2, offs3, offs4):
    idx = unstriped(offs)
    idx2 = unstriped(offs2)
    idx3 = unstriped(offs3)
    idx4 = unstriped(offs4)
    wu = unpack_weight(w_words, w_scales, "e5m2")
    wbu = unpack_weight(wb_words, wb_scales, "e2m1")
    u = (f64(xf)[:, idx] - f64(ow)) * f64(fk)
    uq = mxq(u, 0, "e5m2")
    a = wu.T @ uq
    hid = np.maximum(a[:, idx2], a[:, idx3])
    hidq = mxq(hid, 0, "e5m2")
    p = wbu.T @ hidq
    y = p * f64(tz)[:, idx4]
    words, scales = planes(y)
    return y, words, scales

@@ -1,0 +1,154 @@
+from contextlib import ExitStack
+
+import concourse.mybir as mybir
+
+K, T, J, R, O, N, Z = 512, 512, 256, 512, 128, 512, 512
+FLOPS = 2 * K * R * J + 2 * R * N * O
+
+F32 = mybir.dt.float32
+BF16 = mybir.dt.bfloat16
+I32 = mybir.dt.int32
+U32 = mybir.dt.uint32
+U16 = mybir.dt.uint16
+U8 = mybir.dt.uint8
+E5M2X4 = mybir.dt.float8_e5m2_x4
+E4M3X4 = mybir.dt.float8_e4m3fn_x4
+E2M1X4 = mybir.dt.float4_e2m1fn_x4
+ALU = mybir.AluOpType
+COPY = mybir.ActivationFunctionType.Copy
+
+P = 128
+PACK = 4
+LIST_ROWS = 16
+RUN = 4
+
+
+def load_scale_rows(queue, tile, scales):
+    for q in range(4):
+        queue.dma_start(out=tile[32 * q : 32 * q + 4, :].bitcast(I32), in_=scales[0, 4 * q : 4 * q + 4, :].bitcast(I32))
+
+
+def tile_list_looks_offsetpicks_larger_timeslook_pl_kernel(
+    tc, xf, ow, fk, w_words, w_scales, wb_words, wb_scales, tz, offs, offs2, offs3, offs4, out_0, out_1, out_2
+):
+    nc = tc.nc
+    with ExitStack() as ctx:
+        sb = ctx.enter_context(tc.tile_pool(name="sb", bufs=1))
+        psum = ctx.enter_context(tc.psum_pool(name="psum", bufs=1))
+
+        def tile(name, shape, dtype):
+            return sb.tile(shape, dtype, name=name, align_bytes=64)
+
+        idx = tile("idx", [P, J // LIST_ROWS], U16)
+        idx2 = tile("idx2", [P, O // LIST_ROWS], U16)
+        idx3 = tile("idx3", [P, O // LIST_ROWS], U16)
+        idx4 = tile("idx4", [P, O // LIST_ROWS], U16)
+        fk_sb = tile("fk_sb", [P, PACK], F32)
+        x_sb = [tile(f"x{t}", [P, T], F32) for t in range(PACK)]
+        ow_sb = [tile(f"ow{h}", [P, 2, J], F32) for h in range(2)]
+        tz_sb = tile("tz_sb", [P, PACK, Z], F32)
+        w_raw = tile("w_raw", [P, R], U32)
+        ws_raw = tile("ws_raw", [P, R], U8)
+        wb_raw = tile("wb_raw", [P, N], U16)
+        wbs_raw = tile("wbs_raw", [P, N], U8)
+
+        nc.vector.memset(ws_raw[:].bitcast(I32), 0)
+        nc.vector.memset(wbs_raw[:].bitcast(I32), 0)
+
+        xf_v = xf.rearrange("(p t) c -> p t c", t=PACK)
+        ow_v = ow.rearrange("(p t) c -> p t c", t=PACK)
+        nc.sync.dma_start(idx[:], offs)
+        nc.sync.dma_start(out=x_sb[0][:], in_=xf_v[:, 0, :])
+        nc.sync.dma_start(out=ow_sb[0][:], in_=ow_v[:, 0:2, :])
+        nc.scalar.dma_start(out=fk_sb[:], in_=fk.rearrange("(p t) o -> p (t o)", t=PACK))
+        load_scale_rows(nc.gpsimd, ws_raw, w_scales)
+        nc.sync.dma_start(out=x_sb[1][:], in_=xf_v[:, 1, :])
+        nc.sync.dma_start(out=x_sb[2][:], in_=xf_v[:, 2, :])
+        nc.sync.dma_start(out=ow_sb[1][:], in_=ow_v[:, 2:4, :])
+        nc.sync.dma_start(out=x_sb[3][:], in_=xf_v[:, 3, :])
+        nc.sync.dma_start(idx2[:], offs2)
+        nc.sync.dma_start(idx3[:], offs3)
+        nc.sync.dma_start(out=w_raw[:].bitcast(I32), in_=w_words[0].rearrange("p c r -> p (c r)").bitcast(I32))
+        nc.sync.dma_start(out=wb_raw[:].bitcast(I32), in_=wb_words[0].bitcast(I32))
+        load_scale_rows(nc.sync, wbs_raw, wb_scales)
+        nc.sync.dma_start(idx4[:], offs4)
+        nc.sync.dma_start(out=tz_sb[:], in_=tz.rearrange("(p t) c -> p t c", t=PACK))
+
+        u_bf = tile("u_bf", [P, J, PACK], BF16)
+        pieces = [(0, 0, J), (1, 0, J), (2, 0, J), (3, 0, J // 2), (3, J // 2, J)]
+        ws = tile("ws", [P, R], U8)
+        for t, j0, j1 in pieces:
+            diff = tile(f"diff{t}_{j0}", [P, j1 - j0], F32)
+            picked = x_sb[t][:].indirect(idx[:, j0 // LIST_ROWS : j1 // LIST_ROWS])
+            nc.vector.tensor_tensor(diff[:], picked, ow_sb[t // 2][:, t % 2, j0:j1], ALU.subtract)
+            nc.scalar.activation(out=u_bf[:, j0:j1, t], in_=diff[:], func=COPY, scale=fk_sb[:, t : t + 1])
+
+        nc.vector.tensor_copy(out=ws[:].rearrange("p (t m) -> p t m", t=PACK), in_=ws_raw[:].rearrange("p (m t) -> p t m", t=PACK))
+        w = tile("w", [P, R], U32)
+        nc.vector.tensor_copy(
+            out=w[:].rearrange("p (t c i) -> p c t i", t=PACK, i=RUN),
+            in_=w_raw[:].rearrange("p (c i t) -> p c t i", t=PACK, i=RUN),
+        )
+        u_q = tile("u_q", [P, J], U32)
+        u_s = tile("u_s", [P, J], U8)
+        nc.vector.quantize_mx(out=u_q[:].bitcast(E5M2X4), scales=u_s[:], in_=u_bf[:].rearrange("p j t -> p (j t)"))
+
+        wb = tile("wb", [P, N], U16)
+        wbs = tile("wbs", [P, N], U8)
+        nc.vector.tensor_copy(out=wb[:].rearrange("p (t m) -> p t m", t=PACK), in_=wb_raw[:].rearrange("p (m t) -> p t m", t=PACK))
+        nc.vector.tensor_copy(out=wbs[:].rearrange("p (t m) -> p t m", t=PACK), in_=wbs_raw[:].rearrange("p (m t) -> p t m", t=PACK))
+
+        a2 = tile("a2", [P, PACK, O], F32)
+        a3 = tile("a3", [P, PACK, O], F32)
+        for t in range(PACK):
+            cols = slice(t * P, (t + 1) * P)
+            a_ps = psum.tile([P, J], F32, name=f"a_ps{t}")
+            nc.tensor.matmul_mx(
+                out=a_ps[:], lhsT=w[:, cols].bitcast(E5M2X4), lhsT_scale=ws[:, cols],
+                rhs=u_q[:].bitcast(E5M2X4), rhs_scale=u_s[:], start=True, stop=True,
+            )
+            a_sb = tile(f"a_sb{t}", [P, J], F32)
+            if t % 2 == 0:
+                nc.vector.tensor_copy(out=a_sb[:], in_=a_ps[:])
+            else:
+                nc.scalar.copy(out=a_sb[:], in_=a_ps[:])
+            nc.vector.tensor_copy(out=a2[:, t, :], in_=a_sb[:].indirect(idx2[:]))
+            nc.scalar.activation(out=a3[:, t, :], in_=a_sb[:].indirect(idx3[:]), func=COPY)
+
+        hid_bf = tile("hid_bf", [P, O * PACK], BF16)
+        nc.vector.tensor_tensor(
+            hid_bf[:].rearrange("p (c i t) -> p c t i", t=PACK, i=RUN),
+            a2[:].rearrange("p t (c i) -> p c t i", i=RUN),
+            a3[:].rearrange("p t (c i) -> p c t i", i=RUN),
+            ALU.max,
+        )
+        hid_q = tile("hid_q", [P, O], U32)
+        hid_s = tile("hid_s", [P, O], U8)
+        nc.vector.quantize_mx(out=hid_q[:].bitcast(E5M2X4), scales=hid_s[:], in_=hid_bf[:])
+
+        tz4 = tile("tz4", [P, PACK, O], F32)
+        for t in range(PACK):
+            nc.scalar.activation(out=tz4[:, t, :], in_=tz_sb[:, t, :].indirect(idx4[:]), func=COPY)
+
+        p_ps = psum.tile([P, PACK, O], F32, name="p_ps")
+        for t in range(PACK):
+            cols = slice(t * P, (t + 1) * P)
+            nc.tensor.matmul_mx(
+                out=p_ps[:, t, :], lhsT=wb[:, cols].bitcast(E2M1X4), lhsT_scale=wbs[:, cols],
+                rhs=hid_q[:].bitcast(E5M2X4), rhs_scale=hid_s[:], start=True, stop=True,
+            )
+        y = tile("y", [P, PACK, O], F32)
+        nc.vector.tensor_tensor(y[:], p_ps[:], tz4[:], ALU.mult)
+        nc.sync.dma_start(out=out_0.rearrange("(p t) o -> p t o", t=PACK), in_=y[:])
+        y_bf = tile("y_bf", [P, O * PACK], BF16)
+        nc.vector.tensor_copy(
+            out=y_bf[:].rearrange("p (c i t) -> p c t i", t=PACK, i=RUN),
+            in_=y[:].rearrange("p t (c i) -> p c t i", i=RUN),
+        )
+        y_q = tile("y_q", [P, O], U32)
+        y_s = tile("y_s", [P, O], U8)
+        nc.vector.quantize_mx(out=y_q[:].bitcast(E4M3X4), scales=y_s[:], in_=y_bf[:])
+        nc.sync.dma_start(out=out_1[0].rearrange("p c r -> p (c r)").bitcast(I32), in_=y_q[:].bitcast(I32))
+        for q in range(4):
+            queue = nc.scalar if q % 2 == 0 else nc.sync
+            queue.dma_start(out=out_2[0, 4 * q : 4 * q + 4, :].bitcast(I32), in_=y_s[32 * q : 32 * q + 4, :].bitcast(I32))

@@ -20,7 +20,9 @@ COPY = mybir.ActivationFunctionType.Copy
 P = 128
 PACK = 4
 LIST_ROWS = 16
-RUN = 4
+RUN = 2
+HALF = J // 2
+OH = O // 2
 
 
 def load_scale_rows(queue, tile, scales):
@@ -36,8 +38,8 @@ def tile_list_looks_offsetpicks_larger_timeslook_pl_kernel(
         sb = ctx.enter_context(tc.tile_pool(name="sb", bufs=1))
         psum = ctx.enter_context(tc.psum_pool(name="psum", bufs=1))
 
-        def tile(name, shape, dtype):
-            return sb.tile(shape, dtype, name=name, align_bytes=64)
+        def tile(name, shape, dtype, tag=None):
+            return sb.tile(shape, dtype, name=name, tag=tag or name, align_bytes=64)
 
         idx = tile("idx", [P, J // LIST_ROWS], U16)
         idx2 = tile("idx2", [P, O // LIST_ROWS], U16)
@@ -46,108 +48,145 @@ def tile_list_looks_offsetpicks_larger_timeslook_pl_kernel(
         fk_sb = tile("fk_sb", [P, PACK], F32)
         x_sb = [tile(f"x{t}", [P, T], F32) for t in range(PACK)]
         ow_sb = [tile(f"ow{h}", [P, 2, J], F32) for h in range(2)]
-        tz_sb = tile("tz_sb", [P, PACK, Z], F32)
         w_raw = tile("w_raw", [P, R], U32)
         ws_raw = tile("ws_raw", [P, R], U8)
-        wb_raw = tile("wb_raw", [P, N], U16)
-        wbs_raw = tile("wbs_raw", [P, N], U8)
 
         nc.vector.memset(ws_raw[:].bitcast(I32), 0)
-        nc.vector.memset(wbs_raw[:].bitcast(I32), 0)
 
+        warm_in = tile("warm_in", [P, 1], F32)
+        warm_out = tile("warm_out", [P, 1], F32)
+        nc.gpsimd.memset(warm_in[:], 0.0)
+        nc.scalar.activation(out=warm_out[:], in_=warm_in[:], func=COPY)
         xf_v = xf.rearrange("(p t) c -> p t c", t=PACK)
         ow_v = ow.rearrange("(p t) c -> p t c", t=PACK)
         nc.sync.dma_start(idx[:], offs)
-        nc.sync.dma_start(out=x_sb[0][:], in_=xf_v[:, 0, :])
-        nc.sync.dma_start(out=ow_sb[0][:], in_=ow_v[:, 0:2, :])
         nc.scalar.dma_start(out=fk_sb[:], in_=fk.rearrange("(p t) o -> p (t o)", t=PACK))
-        load_scale_rows(nc.gpsimd, ws_raw, w_scales)
+        nc.sync.dma_start(out=x_sb[0][:], in_=xf_v[:, 0, :])
+        nc.sync.dma_start(idx2[:], offs2)
+        nc.sync.dma_start(idx3[:], offs3)
+        nc.sync.dma_start(out=ow_sb[0][:], in_=ow_v[:, 0:2, :])
         nc.sync.dma_start(out=x_sb[1][:], in_=xf_v[:, 1, :])
         nc.sync.dma_start(out=x_sb[2][:], in_=xf_v[:, 2, :])
         nc.sync.dma_start(out=ow_sb[1][:], in_=ow_v[:, 2:4, :])
         nc.sync.dma_start(out=x_sb[3][:], in_=xf_v[:, 3, :])
-        nc.sync.dma_start(idx2[:], offs2)
-        nc.sync.dma_start(idx3[:], offs3)
         nc.sync.dma_start(out=w_raw[:].bitcast(I32), in_=w_words[0].rearrange("p c r -> p (c r)").bitcast(I32))
-        nc.sync.dma_start(out=wb_raw[:].bitcast(I32), in_=wb_words[0].bitcast(I32))
-        load_scale_rows(nc.sync, wbs_raw, wb_scales)
         nc.sync.dma_start(idx4[:], offs4)
+        load_scale_rows(nc.sync, ws_raw, w_scales)
+
+        pairs = [tile(f"pairs{h}", [P, 2, HALF, 2], BF16) for h in range(2)]
+        for t in range(PACK):
+            cuts = [(0, J)] if t < PACK - 1 else [(0, HALF), (HALF, J)]
+            for j0, j1 in cuts:
+                diff = tile(f"diff{t}_{j0}", [P, j1 - j0], F32)
+                picked = x_sb[t][:].indirect(idx[:, j0 // LIST_ROWS : j1 // LIST_ROWS])
+                nc.vector.tensor_tensor(diff[:], picked, ow_sb[t // 2][:, t % 2, j0:j1], ALU.subtract)
+
+                for h in range(j0 // HALF, j1 // HALF):
+                    nc.scalar.activation(
+                        out=pairs[h][:, t // 2, :, t % 2], in_=diff[:, h * HALF - j0 : (h + 1) * HALF - j0], func=COPY, scale=fk_sb[:, t : t + 1]
+                    )
+
+        wb_both = tile("wb_both", [P, 3 * N], U8, tag="x0")
+        wb_raw, wbs_raw = wb_both[:, 0 : 2 * N], wb_both[:, 2 * N : 3 * N]
+        nc.sync.dma_start(out=wb_raw.bitcast(I32), in_=wb_words[0].bitcast(I32))
+        nc.gpsimd.memset(wbs_raw.bitcast(I32), 0)
+        load_scale_rows(nc.sync, wbs_raw, wb_scales)
+        tz_sb = tile("tz_sb", [P, PACK, Z], F32, tag="x3")
         nc.sync.dma_start(out=tz_sb[:], in_=tz.rearrange("(p t) c -> p t c", t=PACK))
-
-        u_bf = tile("u_bf", [P, J, PACK], BF16)
-        pieces = [(0, 0, J), (1, 0, J), (2, 0, J), (3, 0, J // 2), (3, J // 2, J)]
-        ws = tile("ws", [P, R], U8)
-        for t, j0, j1 in pieces:
-            diff = tile(f"diff{t}_{j0}", [P, j1 - j0], F32)
-            picked = x_sb[t][:].indirect(idx[:, j0 // LIST_ROWS : j1 // LIST_ROWS])
-            nc.vector.tensor_tensor(diff[:], picked, ow_sb[t // 2][:, t % 2, j0:j1], ALU.subtract)
-            nc.scalar.activation(out=u_bf[:, j0:j1, t], in_=diff[:], func=COPY, scale=fk_sb[:, t : t + 1])
-
-        nc.vector.tensor_copy(out=ws[:].rearrange("p (t m) -> p t m", t=PACK), in_=ws_raw[:].rearrange("p (m t) -> p t m", t=PACK))
         w = tile("w", [P, R], U32)
+        ws = tile("ws", [P, R], U8)
         nc.vector.tensor_copy(
-            out=w[:].rearrange("p (t c i) -> p c t i", t=PACK, i=RUN),
-            in_=w_raw[:].rearrange("p (c i t) -> p c t i", t=PACK, i=RUN),
+            out=w[:].rearrange("p (t c i) -> p c t i", t=PACK, i=4),
+            in_=w_raw[:].rearrange("p (c i t) -> p c t i", t=PACK, i=4),
         )
-        u_q = tile("u_q", [P, J], U32)
-        u_s = tile("u_s", [P, J], U8)
-        nc.vector.quantize_mx(out=u_q[:].bitcast(E5M2X4), scales=u_s[:], in_=u_bf[:].rearrange("p j t -> p (j t)"))
+        nc.vector.tensor_copy(out=ws[:].rearrange("p (t m) -> p t m", t=PACK), in_=ws_raw[:].rearrange("p (m t) -> p t m", t=PACK))
+
+        u_all = tile("u_bf", [P, J * PACK], BF16, tag="ws_raw")
+        u_bf, u_q, u_s = [], [], []
+        for h in range(2):
+            u_bf.append(u_all[:, h * HALF * PACK : (h + 1) * HALF * PACK])
+            u_q.append(tile(f"u_q{h}", [P, HALF], U32, tag=None))
+            u_s.append(tile(f"u_s{h}", [P, HALF], U8))
+
+        def weave(h):
+            nc.vector.tensor_copy(
+                out=u_bf[h].bitcast(U32).rearrange("p (j g) -> p j g", g=2),
+                in_=pairs[h][:].rearrange("p g j e -> p (g j e)").bitcast(U32).rearrange("p (g j) -> p j g", g=2),
+            )
+
+        def quantise_u(h):
+            nc.vector.quantize_mx(out=u_q[h][:].bitcast(E5M2X4), scales=u_s[h][:], in_=u_bf[h])
+
+        weave(0)
+        weave(1)
+        quantise_u(0)
+        quantise_u(1)
+
+        a_ps = [psum.tile([P, J], F32, name=f"a_ps{t}") for t in range(PACK)]
+        for h, t in [(0, 0), (0, 1), (1, 0), (1, 1), (0, 2), (1, 2), (0, 3), (1, 3)]:
+            nc.tensor.matmul_mx(
+                out=a_ps[t][:, h * HALF : (h + 1) * HALF], lhsT=w[:, t * P : (t + 1) * P].bitcast(E5M2X4), lhsT_scale=ws[:, t * P : (t + 1) * P],
+                rhs=u_q[h][:].bitcast(E5M2X4), rhs_scale=u_s[h][:], start=True, stop=True,
+            )
 
         wb = tile("wb", [P, N], U16)
         wbs = tile("wbs", [P, N], U8)
-        nc.vector.tensor_copy(out=wb[:].rearrange("p (t m) -> p t m", t=PACK), in_=wb_raw[:].rearrange("p (m t) -> p t m", t=PACK))
-        nc.vector.tensor_copy(out=wbs[:].rearrange("p (t m) -> p t m", t=PACK), in_=wbs_raw[:].rearrange("p (m t) -> p t m", t=PACK))
+        nc.vector.tensor_copy(out=wb[:].rearrange("p (t m) -> p t m", t=PACK), in_=wb_raw.bitcast(U16).rearrange("p (m t) -> p t m", t=PACK))
+        nc.vector.tensor_copy(out=wbs[:].rearrange("p (t m) -> p t m", t=PACK), in_=wbs_raw.rearrange("p (m t) -> p t m", t=PACK))
 
-        a2 = tile("a2", [P, PACK, O], F32)
-        a3 = tile("a3", [P, PACK, O], F32)
+        a_by2 = tile("a_by2", [P, PACK, O], F32, tag="x0")
+        a_by3 = tile("a_by3", [P, PACK, O], F32)
+        a_sb = [tile(f"a_sb{t}", [P, J], F32) for t in range(PACK)]
         for t in range(PACK):
-            cols = slice(t * P, (t + 1) * P)
-            a_ps = psum.tile([P, J], F32, name=f"a_ps{t}")
-            nc.tensor.matmul_mx(
-                out=a_ps[:], lhsT=w[:, cols].bitcast(E5M2X4), lhsT_scale=ws[:, cols],
-                rhs=u_q[:].bitcast(E5M2X4), rhs_scale=u_s[:], start=True, stop=True,
-            )
-            a_sb = tile(f"a_sb{t}", [P, J], F32)
-            if t % 2 == 0:
-                nc.vector.tensor_copy(out=a_sb[:], in_=a_ps[:])
+            nc.scalar.copy(out=a_sb[t][:], in_=a_ps[t][:])
+        for t in range(PACK):
+            nc.vector.tensor_copy(out=a_by2[:, t, :], in_=a_sb[t][:].indirect(idx2[:]))
+            if t >= 2:
+                nc.vector.tensor_copy(out=a_by3[:, t, :], in_=a_sb[t][:].indirect(idx3[:]))
             else:
-                nc.scalar.copy(out=a_sb[:], in_=a_ps[:])
-            nc.vector.tensor_copy(out=a2[:, t, :], in_=a_sb[:].indirect(idx2[:]))
-            nc.scalar.activation(out=a3[:, t, :], in_=a_sb[:].indirect(idx3[:]), func=COPY)
+                nc.scalar.activation(out=a_by3[:, t, :], in_=a_sb[t][:].indirect(idx3[:]), func=COPY)
 
-        hid_bf = tile("hid_bf", [P, O * PACK], BF16)
-        nc.vector.tensor_tensor(
-            hid_bf[:].rearrange("p (c i t) -> p c t i", t=PACK, i=RUN),
-            a2[:].rearrange("p t (c i) -> p c t i", i=RUN),
-            a3[:].rearrange("p t (c i) -> p c t i", i=RUN),
-            ALU.max,
-        )
         hid_q = tile("hid_q", [P, O], U32)
         hid_s = tile("hid_s", [P, O], U8)
-        nc.vector.quantize_mx(out=hid_q[:].bitcast(E5M2X4), scales=hid_s[:], in_=hid_bf[:])
+        hid_bf = [tile(f"hid_bf{h}", [P, OH * PACK], BF16) for h in range(2)]
+        for h in range(2):
+            places = slice(h * OH, (h + 1) * OH)
+            nc.vector.tensor_tensor(
+                hid_bf[h][:].rearrange("p (c i t) -> p c t i", t=PACK, i=RUN),
+                a_by2[:, :, places].rearrange("p t (c i) -> p c t i", i=RUN),
+                a_by3[:, :, places].rearrange("p t (c i) -> p c t i", i=RUN),
+                ALU.max,
+            )
 
-        tz4 = tile("tz4", [P, PACK, O], F32)
+        for h in range(2):
+            places = slice(h * OH, (h + 1) * OH)
+            nc.vector.quantize_mx(out=hid_q[:, places].bitcast(E5M2X4), scales=hid_s[:, places], in_=hid_bf[h][:])
+
+        tz_by4 = tile("tz_by4", [P, PACK, O], F32, tag="a_sb1")
         for t in range(PACK):
-            nc.scalar.activation(out=tz4[:, t, :], in_=tz_sb[:, t, :].indirect(idx4[:]), func=COPY)
+            nc.scalar.activation(out=tz_by4[:, t, :], in_=tz_sb[:, t, :].indirect(idx4[:]), func=COPY)
 
-        p_ps = psum.tile([P, PACK, O], F32, name="p_ps")
+        y = tile("y", [P, PACK, O], F32)
         for t in range(PACK):
             cols = slice(t * P, (t + 1) * P)
+            p_ps = psum.tile([P, O], F32, name=f"p_ps{t}")
             nc.tensor.matmul_mx(
-                out=p_ps[:, t, :], lhsT=wb[:, cols].bitcast(E2M1X4), lhsT_scale=wbs[:, cols],
+                out=p_ps[:], lhsT=wb[:, cols].bitcast(E2M1X4), lhsT_scale=wbs[:, cols],
                 rhs=hid_q[:].bitcast(E5M2X4), rhs_scale=hid_s[:], start=True, stop=True,
             )
-        y = tile("y", [P, PACK, O], F32)
-        nc.vector.tensor_tensor(y[:], p_ps[:], tz4[:], ALU.mult)
+            nc.vector.tensor_tensor(y[:, t, :], p_ps[:], tz_by4[:, t, :], ALU.mult)
         nc.sync.dma_start(out=out_0.rearrange("(p t) o -> p t o", t=PACK), in_=y[:])
-        y_bf = tile("y_bf", [P, O * PACK], BF16)
-        nc.vector.tensor_copy(
-            out=y_bf[:].rearrange("p (c i t) -> p c t i", t=PACK, i=RUN),
-            in_=y[:].rearrange("p t (c i) -> p c t i", i=RUN),
-        )
         y_q = tile("y_q", [P, O], U32)
         y_s = tile("y_s", [P, O], U8)
-        nc.vector.quantize_mx(out=y_q[:].bitcast(E4M3X4), scales=y_s[:], in_=y_bf[:])
+        y_bf = [tile(f"y_bf{h}", [P, OH * PACK], BF16) for h in range(2)]
+        for h in range(2):
+            nc.vector.tensor_copy(
+                out=y_bf[h][:].rearrange("p (c i t) -> p c t i", t=PACK, i=RUN),
+                in_=y[:, :, h * OH : (h + 1) * OH].rearrange("p t (c i) -> p c t i", i=RUN),
+            )
+        for h in range(2):
+            places = slice(h * OH, (h + 1) * OH)
+            nc.vector.quantize_mx(out=y_q[:, places].bitcast(E4M3X4), scales=y_s[:, places], in_=y_bf[h][:])
         nc.sync.dma_start(out=out_1[0].rearrange("p c r -> p (c r)").bitcast(I32), in_=y_q[:].bitcast(I32))
         for q in range(4):
             queue = nc.scalar if q % 2 == 0 else nc.sync

@@ -134,8 +134,8 @@ def tile_list_looks_offsetpicks_larger_timeslook_pl_kernel(
         nc.vector.tensor_copy(out=wb[:].rearrange("p (t m) -> p t m", t=PACK), in_=wb_raw.bitcast(U16).rearrange("p (m t) -> p t m", t=PACK))
         nc.vector.tensor_copy(out=wbs[:].rearrange("p (t m) -> p t m", t=PACK), in_=wbs_raw.rearrange("p (m t) -> p t m", t=PACK))
 
-        a_by2 = tile("a_by2", [P, PACK, O], F32, tag="x0")
-        a_by3 = tile("a_by3", [P, PACK, O], F32)
+        a_by = tile("a_by", [P, 2, PACK, O], F32, tag="x0")
+        a_by2, a_by3 = a_by[:, 0], a_by[:, 1]
         a_sb = [tile(f"a_sb{t}", [P, J], F32) for t in range(PACK)]
         for t in range(PACK):
             nc.scalar.copy(out=a_sb[t][:], in_=a_ps[t][:])

from contextlib import ExitStack

import concourse.mybir as mybir

K, T, J, R, O, N, Z = 512, 512, 256, 512, 128, 512, 512
FLOPS = 2 * K * R * J + 2 * R * N * O

F32 = mybir.dt.float32
BF16 = mybir.dt.bfloat16
I32 = mybir.dt.int32
U32 = mybir.dt.uint32
U16 = mybir.dt.uint16
U8 = mybir.dt.uint8
E5M2X4 = mybir.dt.float8_e5m2_x4
E4M3X4 = mybir.dt.float8_e4m3fn_x4
E2M1X4 = mybir.dt.float4_e2m1fn_x4
ALU = mybir.AluOpType
COPY = mybir.ActivationFunctionType.Copy

P = 128
PACK = 4
LIST_ROWS = 16
RUN = 2
HALF = J // 2
OH = O // 2


def load_scale_rows(queue, tile, scales):
    for q in range(4):
        queue.dma_start(out=tile[32 * q : 32 * q + 4, :].bitcast(I32), in_=scales[0, 4 * q : 4 * q + 4, :].bitcast(I32))


def tile_list_looks_offsetpicks_larger_timeslook_pl_kernel(
    tc, xf, ow, fk, w_words, w_scales, wb_words, wb_scales, tz, offs, offs2, offs3, offs4, out_0, out_1, out_2
):
    nc = tc.nc
    with ExitStack() as ctx:
        sb = ctx.enter_context(tc.tile_pool(name="sb", bufs=1))
        psum = ctx.enter_context(tc.psum_pool(name="psum", bufs=1))

        def tile(name, shape, dtype, tag=None):
            return sb.tile(shape, dtype, name=name, tag=tag or name, align_bytes=64)

        idx = tile("idx", [P, J // LIST_ROWS], U16)
        idx2 = tile("idx2", [P, O // LIST_ROWS], U16)
        idx3 = tile("idx3", [P, O // LIST_ROWS], U16)
        idx4 = tile("idx4", [P, O // LIST_ROWS], U16)
        fk_sb = tile("fk_sb", [P, PACK], F32)
        x_sb = [tile(f"x{t}", [P, T], F32) for t in range(PACK)]
        ow_sb = [tile(f"ow{h}", [P, 2, J], F32) for h in range(2)]
        w_raw = tile("w_raw", [P, R], U32)
        ws_raw = tile("ws_raw", [P, R], U8)

        nc.vector.memset(ws_raw[:].bitcast(I32), 0)

        warm_in = tile("warm_in", [P, 1], F32)
        warm_out = tile("warm_out", [P, 1], F32)
        nc.gpsimd.memset(warm_in[:], 0.0)
        nc.scalar.activation(out=warm_out[:], in_=warm_in[:], func=COPY)
        xf_v = xf.rearrange("(p t) c -> p t c", t=PACK)
        ow_v = ow.rearrange("(p t) c -> p t c", t=PACK)
        nc.sync.dma_start(idx[:], offs)
        nc.scalar.dma_start(out=fk_sb[:], in_=fk.rearrange("(p t) o -> p (t o)", t=PACK))
        nc.sync.dma_start(out=x_sb[0][:], in_=xf_v[:, 0, :])
        nc.sync.dma_start(idx2[:], offs2)
        nc.sync.dma_start(idx3[:], offs3)
        nc.sync.dma_start(out=ow_sb[0][:], in_=ow_v[:, 0:2, :])
        nc.sync.dma_start(out=x_sb[1][:], in_=xf_v[:, 1, :])
        nc.sync.dma_start(out=x_sb[2][:], in_=xf_v[:, 2, :])
        nc.sync.dma_start(out=ow_sb[1][:], in_=ow_v[:, 2:4, :])
        nc.sync.dma_start(out=x_sb[3][:], in_=xf_v[:, 3, :])
        nc.sync.dma_start(out=w_raw[:].bitcast(I32), in_=w_words[0].rearrange("p c r -> p (c r)").bitcast(I32))
        nc.sync.dma_start(idx4[:], offs4)
        load_scale_rows(nc.sync, ws_raw, w_scales)

        pairs = [tile(f"pairs{h}", [P, 2, HALF, 2], BF16) for h in range(2)]
        for t in range(PACK):
            cuts = [(0, J)] if t < PACK - 1 else [(0, HALF), (HALF, J)]
            for j0, j1 in cuts:
                diff = tile(f"diff{t}_{j0}", [P, j1 - j0], F32)
                picked = x_sb[t][:].indirect(idx[:, j0 // LIST_ROWS : j1 // LIST_ROWS])
                nc.vector.tensor_tensor(diff[:], picked, ow_sb[t // 2][:, t % 2, j0:j1], ALU.subtract)

                for h in range(j0 // HALF, j1 // HALF):
                    nc.scalar.activation(
                        out=pairs[h][:, t // 2, :, t % 2], in_=diff[:, h * HALF - j0 : (h + 1) * HALF - j0], func=COPY, scale=fk_sb[:, t : t + 1]
                    )

        wb_both = tile("wb_both", [P, 3 * N], U8, tag="x0")
        wb_raw, wbs_raw = wb_both[:, 0 : 2 * N], wb_both[:, 2 * N : 3 * N]
        nc.sync.dma_start(out=wb_raw.bitcast(I32), in_=wb_words[0].bitcast(I32))
        nc.gpsimd.memset(wbs_raw.bitcast(I32), 0)
        load_scale_rows(nc.sync, wbs_raw, wb_scales)
        tz_sb = tile("tz_sb", [P, PACK, Z], F32, tag="x3")
        nc.sync.dma_start(out=tz_sb[:], in_=tz.rearrange("(p t) c -> p t c", t=PACK))
        w = tile("w", [P, R], U32)
        ws = tile("ws", [P, R], U8)
        nc.vector.tensor_copy(
            out=w[:].rearrange("p (t c i) -> p c t i", t=PACK, i=4),
            in_=w_raw[:].rearrange("p (c i t) -> p c t i", t=PACK, i=4),
        )
        nc.vector.tensor_copy(out=ws[:].rearrange("p (t m) -> p t m", t=PACK), in_=ws_raw[:].rearrange("p (m t) -> p t m", t=PACK))

        u_all = tile("u_bf", [P, J * PACK], BF16, tag="ws_raw")
        u_bf, u_q, u_s = [], [], []
        for h in range(2):
            u_bf.append(u_all[:, h * HALF * PACK : (h + 1) * HALF * PACK])
            u_q.append(tile(f"u_q{h}", [P, HALF], U32, tag=None))
            u_s.append(tile(f"u_s{h}", [P, HALF], U8))

        def weave(h):
            nc.vector.tensor_copy(
                out=u_bf[h].bitcast(U32).rearrange("p (j g) -> p j g", g=2),
                in_=pairs[h][:].rearrange("p g j e -> p (g j e)").bitcast(U32).rearrange("p (g j) -> p j g", g=2),
            )

        def quantise_u(h):
            nc.vector.quantize_mx(out=u_q[h][:].bitcast(E5M2X4), scales=u_s[h][:], in_=u_bf[h])

        weave(0)
        weave(1)
        quantise_u(0)
        quantise_u(1)

        a_ps = [psum.tile([P, J], F32, name=f"a_ps{t}") for t in range(PACK)]
        for h, t in [(0, 0), (0, 1), (1, 0), (1, 1), (0, 2), (1, 2), (0, 3), (1, 3)]:
            nc.tensor.matmul_mx(
                out=a_ps[t][:, h * HALF : (h + 1) * HALF], lhsT=w[:, t * P : (t + 1) * P].bitcast(E5M2X4), lhsT_scale=ws[:, t * P : (t + 1) * P],
                rhs=u_q[h][:].bitcast(E5M2X4), rhs_scale=u_s[h][:], start=True, stop=True,
            )

        wb = tile("wb", [P, N], U16)
        wbs = tile("wbs", [P, N], U8)
        nc.vector.tensor_copy(out=wb[:].rearrange("p (t m) -> p t m", t=PACK), in_=wb_raw.bitcast(U16).rearrange("p (m t) -> p t m", t=PACK))
        nc.vector.tensor_copy(out=wbs[:].rearrange("p (t m) -> p t m", t=PACK), in_=wbs_raw.rearrange("p (m t) -> p t m", t=PACK))

        a_by = tile("a_by", [P, 2, PACK, O], F32, tag="x0")
        a_by2, a_by3 = a_by[:, 0], a_by[:, 1]
        a_sb = [tile(f"a_sb{t}", [P, J], F32) for t in range(PACK)]
        for t in range(PACK):
            nc.scalar.copy(out=a_sb[t][:], in_=a_ps[t][:])
        for t in range(PACK):
            nc.vector.tensor_copy(out=a_by2[:, t, :], in_=a_sb[t][:].indirect(idx2[:]))
            if t >= 2:
                nc.vector.tensor_copy(out=a_by3[:, t, :], in_=a_sb[t][:].indirect(idx3[:]))
            else:
                nc.scalar.activation(out=a_by3[:, t, :], in_=a_sb[t][:].indirect(idx3[:]), func=COPY)

        hid_q = tile("hid_q", [P, O], U32)
        hid_s = tile("hid_s", [P, O], U8)
        hid_bf = [tile(f"hid_bf{h}", [P, OH * PACK], BF16) for h in range(2)]
        for h in range(2):
            places = slice(h * OH, (h + 1) * OH)
            nc.vector.tensor_tensor(
                hid_bf[h][:].rearrange("p (c i t) -> p c t i", t=PACK, i=RUN),
                a_by2[:, :, places].rearrange("p t (c i) -> p c t i", i=RUN),
                a_by3[:, :, places].rearrange("p t (c i) -> p c t i", i=RUN),
                ALU.max,
            )

        for h in range(2):
            places = slice(h * OH, (h + 1) * OH)
            nc.vector.quantize_mx(out=hid_q[:, places].bitcast(E5M2X4), scales=hid_s[:, places], in_=hid_bf[h][:])

        tz_by4 = tile("tz_by4", [P, PACK, O], F32, tag="a_sb1")
        for t in range(PACK):
            nc.scalar.activation(out=tz_by4[:, t, :], in_=tz_sb[:, t, :].indirect(idx4[:]), func=COPY)

        y = tile("y", [P, PACK, O], F32)
        for t in range(PACK):
            cols = slice(t * P, (t + 1) * P)
            p_ps = psum.tile([P, O], F32, name=f"p_ps{t}")
            nc.tensor.matmul_mx(
                out=p_ps[:], lhsT=wb[:, cols].bitcast(E2M1X4), lhsT_scale=wbs[:, cols],
                rhs=hid_q[:].bitcast(E5M2X4), rhs_scale=hid_s[:], start=True, stop=True,
            )
            nc.vector.tensor_tensor(y[:, t, :], p_ps[:], tz_by4[:, t, :], ALU.mult)
        nc.sync.dma_start(out=out_0.rearrange("(p t) o -> p t o", t=PACK), in_=y[:])
        y_q = tile("y_q", [P, O], U32)
        y_s = tile("y_s", [P, O], U8)
        y_bf = [tile(f"y_bf{h}", [P, OH * PACK], BF16) for h in range(2)]
        for h in range(2):
            nc.vector.tensor_copy(
                out=y_bf[h][:].rearrange("p (c i t) -> p c t i", t=PACK, i=RUN),
                in_=y[:, :, h * OH : (h + 1) * OH].rearrange("p t (c i) -> p c t i", i=RUN),
            )
        for h in range(2):
            places = slice(h * OH, (h + 1) * OH)
            nc.vector.quantize_mx(out=y_q[:, places].bitcast(E4M3X4), scales=y_s[:, places], in_=y_bf[h][:])
        nc.sync.dma_start(out=out_1[0].rearrange("p c r -> p (c r)").bitcast(I32), in_=y_q[:].bitcast(I32))
        for q in range(4):
            queue = nc.scalar if q % 2 == 0 else nc.sync
            queue.dma_start(out=out_2[0, 4 * q : 4 * q + 4, :].bitcast(I32), in_=y_s[32 * q : 32 * q + 4, :].bitcast(I32))
